import numpy as np
import ml_dtypes


def mxq(x, axis, fmt="e4m3"):
    dtype, down = {"e4m3": (ml_dtypes.float8_e4m3fn, 7), "e5m2": (ml_dtypes.float8_e5m2, 14)}[fmt]
    v = np.moveaxis(np.asarray(x, np.float32).astype(ml_dtypes.bfloat16).astype(np.float64), axis, -1)
    blocks = v.reshape(v.shape[:-1] + (-1, 32))
    amax = np.abs(blocks).max(-1, keepdims=True)
    byte = np.maximum(np.where(amax > 0, np.frexp(amax)[1] - 1 + 127, 0) - down, 1)
    scale = np.exp2(byte - 127.0)
    codes = (blocks / scale).astype(np.float32).astype(dtype).astype(np.float64)
    return np.moveaxis((codes * scale).reshape(v.shape), -1, axis)


WIDE = False


def mx_kscale(k):
    if not WIDE:
        return np.ones(k)
    levels = np.array([10, -10, 5, -5, 0])
    if k % 512:
        return np.exp2(np.random.permutation(np.resize(levels, k // 32))).repeat(32)
    a = np.empty((k // 512, 16))
    for p in range(k // 512):
        a[p, :8] = np.random.permutation(np.resize(levels, 8))
        for g in range(8):
            far = levels[np.abs(levels - a[p, g]) >= 10]
            a[p, g + 8] = far[np.random.randint(len(far))]
    return np.exp2(a.ravel()).repeat(32)


def f64(x):
    return np.asarray(x).astype(np.float64)


def striped(idx):
    return np.tile(idx.reshape(-1, 16).T, (8, 1)).astype(np.uint16)


def unstriped(offs):
    return offs[:16].T.reshape(-1).astype(np.int64)


E2M1 = np.array([0.0, 0.5, 1.0, 1.5, 2.0, 3.0, 4.0, 6.0, -0.0, -0.5, -1.0, -1.5, -2.0, -3.0, -4.0, -6.0])


def pack_weight(w, fmt):
    k, n = w.shape
    w = f64(np.asarray(w, np.float32).astype(ml_dtypes.bfloat16)).reshape(k // 32, 32, n)
    amax = np.abs(w).max(1)
    if fmt == "e4m3":
        byte = np.frexp(amax)[1] - 1 + 127 - 7
    else:
        mant, ex = np.frexp(amax / 6.0)
        byte = np.where(mant > 0.5, ex, ex - 1) + 127
    byte = np.clip(np.where(amax > 0, byte, 1), 1, 254)
    scaled = (w * np.exp2(127.0 - byte)[:, None, :]).reshape(k, n).astype(np.float32)
    by_word = np.ascontiguousarray(scaled.reshape(k // 512, 128, 4, n).transpose(0, 1, 3, 2))
    if fmt == "e4m3":
        words = by_word.astype(ml_dtypes.float8_e4m3fn).view(np.uint8)
    else:
        c = by_word.astype(ml_dtypes.float4_e2m1fn).view(np.uint8) & 0xF
        words = (c[..., 0::2] | (c[..., 1::2] << 4)).reshape(k // 512, 128, 2 * n)
    return np.ascontiguousarray(words), np.ascontiguousarray(byte.astype(np.uint8).reshape(k // 512, 16, n))


def unpack_weight(words, scales, fmt):
    g, _, n = scales.shape
    words = np.ascontiguousarray(words).reshape(g, 128, n, -1)
    if fmt == "e4m3":
        vals = words.view(ml_dtypes.float8_e4m3fn).astype(np.float64)
    else:
        nib = np.empty((g, 128, n, 4), np.uint8)
        nib[..., 0::2] = words & 0xF
        nib[..., 1::2] = words >> 4
        vals = E2M1[nib]
    vals = vals * np.repeat(np.exp2(scales.astype(np.float64) - 127.0), 8, axis=1)[..., None]
    return vals.transpose(0, 1, 3, 2).reshape(g * 512, n)


def gelu(v):
    return 0.5 * v * (1.0 + np.tanh(np.sqrt(2.0 / np.pi) * (v + 0.044715 * v**3)))


K, H, N, T, S, P = 1024, 1024, 512, 4096, 1024, 512

def setup_inputs():
    n = np.random.standard_normal
    s = mx_kscale(K)[:, None]
    u = mx_kscale(H)[:, None]
    tab_words, tab_scales = pack_weight(n((K, T)) * s, "e4m3")
    w4_words, w4_scales = pack_weight(0.9 * n((K, H)) / np.sqrt(K) / s, "e2m1")
    wd = (0.9 * n((K, H)) / np.sqrt(K) / s).astype(np.float32)
    bias = (0.6 * n(H)).astype(np.float32)
    gain = (np.random.uniform(0.6, 1.6, H) * u[:, 0]).astype(np.float32)
    rest = (0.4 * n(H) * u[:, 0]).astype(np.float32)
    bed = (0.7 * n((H, P)) * u).astype(np.float32)
    wa = (1.3 * n((H, N)) / np.sqrt(H) / u).astype(np.float32)
    w8_words, w8_scales = pack_weight(1.2 * n((H, N)) / np.sqrt(H) / u, "e4m3")
    base = (0.6 * n((N, P))).astype(np.float32)
    return {"tab_words": tab_words, "tab_scales": tab_scales,
            "offs": striped(np.random.permutation(T)[:S]),
            "pos1": striped(np.random.permutation(S)[:P]),
            "pos2": striped(np.random.permutation(S)[:P]),
            "w4_words": w4_words, "w4_scales": w4_scales, "wd": wd, "bias": bias, "gain": gain,
            "rest": rest, "bed": bed, "wa": wa, "w8_words": w8_words, "w8_scales": w8_scales, "base": base}

def reference(tab_words, tab_scales, offs, pos1, pos2, w4_words, w4_scales, wd, bias, gain, rest, bed, wa, w8_words, w8_scales, base):
    v = unpack_weight(tab_words, tab_scales, "e4m3")[:, unstriped(offs)]
    w4 = unpack_weight(w4_words, w4_scales, "e2m1")
    w8 = unpack_weight(w8_words, w8_scales, "e4m3")
    pre = w4.T @ v + mxq(f64(wd), 0, "e4m3").T @ v
    h = f64(gain)[:, None] * np.tanh(pre + f64(bias)[:, None])
    xa = np.maximum(h[:, unstriped(pos1)], f64(rest)[:, None])
    xb = h[:, unstriped(pos2)] + f64(bed)
    ya = mxq(f64(wa), 0, "e4m3").T @ mxq(xa, 0, "e4m3")
    yb = w8.T @ mxq(xb, 0, "e4m3")
    return np.maximum(ya * yb, f64(base))

@@ -1,0 +1,319 @@
+from contextlib import ExitStack
+
+import concourse.mybir as mybir
+
+K, H, N, T, S, J = 1024, 1024, 512, 4096, 1024, 512
+FLOPS = 2 * (2 * K * H * S + 2 * H * N * J)
+
+F32 = mybir.dt.float32
+BF16 = mybir.dt.bfloat16
+I32 = mybir.dt.int32
+U32 = mybir.dt.uint32
+U16 = mybir.dt.uint16
+U8 = mybir.dt.uint8
+FP8X4 = mybir.dt.float8_e4m3fn_x4
+FP4X4 = mybir.dt.float4_e2m1fn_x4
+ALU = mybir.AluOpType
+TANH = mybir.ActivationFunctionType.Tanh
+
+P = 128
+PACK = 4
+KP = P * PACK
+BANK = 512
+HALF = J // 2
+
+
+def tile_list_bed_window_scores_kernel(
+    tc, tab_words, tab_scales, offs, pos1, pos2, w4_words, w4_scales, wd, bias, gain, rest, bed, wa,
+    w8_words, w8_scales, base, out,
+):
+    nc = tc.nc
+    with ExitStack() as ctx:
+        lists = ctx.enter_context(tc.tile_pool(name="lists", bufs=1))
+        sb = ctx.enter_context(tc.tile_pool(name="sb", bufs=1))
+        ring = ctx.enter_context(tc.tile_pool(name="ring", bufs=3))
+        psum = ctx.enter_context(tc.psum_pool(name="psum", bufs=1))
+
+        def tile(shape, dtype, name, tag=None):
+            return sb.tile(shape, dtype, name=name, tag=tag or name, align_bytes=64)
+
+        offs_sb = lists.tile([P, S // 16], U16, name="offs_sb")
+        pos1_sb = lists.tile([P, J // 16], U16, name="pos1_sb")
+        pos2_sb = lists.tile([P, J // 16], U16, name="pos2_sb")
+
+        tab_s = tile([P, T], U8, "tab_s")
+        v_s = [tile([P, S], U8, "v_s%d" % a) for a in range(2)]
+        w4s_raw = tile([P, 2 * H], U8, "w4s_raw")
+        w8_s = tile([P, 2 * N], U8, "w8_s")
+        nc.vector.memset(w4s_raw[:].bitcast(I32), 0)
+        nc.vector.memset(tab_s[64:128, :].bitcast(I32), 0)
+        nc.gpsimd.memset(tab_s[32:64, :].bitcast(I32), 0)
+        for a in range(2):
+            nc.gpsimd.memset(v_s[a][:].bitcast(I32), 0)
+        nc.gpsimd.memset(w8_s[:].bitcast(I32), 0)
+
+        def load_scales(queue, plane, scales):
+            for q in range(4):
+                queue.dma_start(
+                    out=plane[32 * q : 32 * q + 4, :].bitcast(I32).rearrange("r (a c) -> r a c", a=2),
+                    in_=scales[:, 4 * q : 4 * q + 4, :].rearrange("a r c -> r a c").bitcast(I32),
+                )
+
+        def load_rows(dst, src, a, cols):
+            nc.sync.dma_start(out=dst, in_=src[a * KP : (a + 1) * KP, cols].rearrange("(p j) c -> p j c", j=PACK))
+
+        tab_w = [tile([P, T], I32, "tab_w%d" % a) for a in range(2)]
+        w4_raw = [tile([P, 2, 256], I32, "w4_raw%d" % b) for b in range(2)]
+        wd_raw = {}
+        wd_raw[0, 0] = tile([P, PACK, KP], F32, "wd_raw00", "raw0")
+        wd_last = tile([P, 2, PACK, KP // 2], F32, "wd_raw01", "raw1")
+        wd_raw[1, 0] = tile([P, PACK, KP], F32, "wd_raw10", "raw2")
+        wd_raw[1, 1] = tile([P, PACK, KP], F32, "wd_raw11", "raw3")
+        bed_sb = [[tile([P, J], F32, "bed%d%d" % (b, t)) for t in range(PACK)] for b in range(2)]
+        w8_w = tile([P, 2 * N], I32, "w8_w")
+        base_sb = tile([P, 4, J], F32, "base_sb")
+
+        def load_tab(a):
+            nc.sync.dma_start(out=tab_w[a][:], in_=tab_words[a].rearrange("p n i -> p (n i)").bitcast(I32))
+
+        def load_w4(b):
+            nc.sync.dma_start(
+                out=w4_raw[b][:],
+                in_=w4_words[:, :, 1024 * b : 1024 * (b + 1)].rearrange("a p c -> p a c").bitcast(I32),
+            )
+
+        def load_bed(b, t):
+            rows = bed[b * KP : (b + 1) * KP, :].rearrange("(p t) j -> p t j", t=PACK)
+            nc.sync.dma_start(out=bed_sb[b][t][:], in_=rows[:, t, :])
+
+        nc.sync.dma_start(offs_sb[:], offs)
+        nc.sync.dma_start(out=tab_s[0:32, :].bitcast(I32), in_=tab_scales.rearrange("a q t -> (a q) t").bitcast(I32))
+        vec = {}
+
+        def load_vec(name, src):
+            vec[name] = tile([P, 2, PACK], F32, name + "_sb")
+            nc.sync.dma_start(out=vec[name][:], in_=src.rearrange("(b p t) -> p b t", b=2, t=PACK))
+
+        load_rows(wd_raw[0, 0][:], wd, 0, slice(0, KP))
+        load_w4(0)
+        load_vec("bias", bias)
+        load_scales(nc.sync, w4s_raw, w4_scales)
+        load_tab(0)
+        load_tab(1)
+        for u in range(2):
+            load_rows(wd_last[:, u], wd, 1, slice(u * 256, (u + 1) * 256))
+        nc.sync.dma_start(pos1_sb[:], pos1)
+        nc.sync.dma_start(pos2_sb[:], pos2)
+        load_vec("gain", gain)
+        load_vec("rest", rest)
+        load_w4(1)
+        load_bed(0, 0)
+        load_rows(wd_raw[1, 0][:], wd, 0, slice(KP, 2 * KP))
+        load_bed(0, 1)
+        load_rows(wd_raw[1, 1][:], wd, 1, slice(KP, 2 * KP))
+        load_bed(0, 2)
+        load_bed(0, 3)
+
+
+        def per_row(name, b, t):
+            return vec[name][:, b, t : t + 1]
+
+        v_w = [tile([P, S], U32, "v_w%d" % a) for a in range(2)]
+
+        def gather_words(a, lo, hi):
+            window = tab_w[a][:].bitcast(U32)
+            nc.vector.tensor_copy(v_w[a][:, lo:hi], window.indirect(offs_sb[:, lo // 16 : hi // 16]))
+
+        picked_s = tile([P, S], U8, "picked_s")
+        nc.vector.tensor_copy(picked_s[:], tab_s[:].indirect(offs_sb[:]))
+        for a in range(2):
+            for q in range(4):
+                row = 16 * a + 4 * q
+                nc.gpsimd.dma_start(
+                    out=v_s[a][32 * q : 32 * q + 4, :].bitcast(I32), in_=picked_s[row : row + 4, :].bitcast(I32)
+                )
+        gather_words(0, 0, S)
+
+        w4_w = tile([P, 4 * KP * 2], U8, "w4_w", "held_b")
+        w4_s = tile([P, 4 * KP], U8, "w4_s")
+        nc.vector.tensor_copy(
+            w4_s[:].rearrange("p (b a t m) -> p b a t m", b=2, a=2, t=PACK),
+            w4s_raw[:].rearrange("p (a b m t) -> p b a t m", a=2, b=2, t=PACK),
+        )
+
+        def deal_w4(b):
+            nc.vector.tensor_copy(
+                w4_w[:, 2048 * b : 2048 * (b + 1)].bitcast(U16).rearrange("p (a t m) -> p a t m", a=2, t=PACK),
+                w4_raw[b][:].bitcast(U16).rearrange("p a (m t) -> p a t m", t=PACK),
+            )
+
+        wd_w = [tile([P, 2 * KP], U32, "wd_w0"), tile([P, 2 * KP], U32, "wd_w1", "held_a")]
+        wd_s = [tile([P, 2 * KP], U8, "wd_s%d" % b) for b in range(2)]
+
+        def quantise(words, scales, woven):
+            nc.vector.quantize_mx(out=words.bitcast(FP8X4), scales=scales, in_=woven)
+
+        def dealt_view(woven):
+            return woven[:].rearrange("p (t m j) -> p m j t", t=PACK, j=PACK)
+
+        def raw_view(raw):
+            return raw.rearrange("p j (m t) -> p m j t", t=PACK)
+
+        def prepare_wd(b, a, tag):
+            woven = tile([P, PACK * KP], BF16, "wd_woven%d%d" % (b, a), tag)
+            nc.scalar.copy(out=dealt_view(woven), in_=raw_view(wd_raw[b, a][:]))
+            cols = slice(a * KP, (a + 1) * KP)
+            quantise(wd_w[b][:, cols], wd_s[b][:, cols], woven[:])
+
+        deal_w4(0)
+        prepare_wd(0, 0, "woven0")
+        gather_words(1, 0, S // 2)
+        gather_words(1, S // 2, S)
+        woven = tile([P, PACK * KP], BF16, "wd_woven01", "woven1")
+        nc.scalar.copy(out=dealt_view(woven)[:, 0:64], in_=raw_view(wd_last[:, 0]))
+        nc.vector.tensor_copy(out=dealt_view(woven)[:, 64:128], in_=raw_view(wd_last[:, 1]))
+        for t in range(PACK):
+            cols = slice(KP + t * P, KP + (t + 1) * P)
+            quantise(wd_w[0][:, cols], wd_s[0][:, cols], woven[:, t * KP : (t + 1) * KP])
+        deal_w4(1)
+
+        act = {}
+
+        def first_stage(b, t, order):
+            act[b, t] = tile([P, S], F32, "act%d%d" % (b, t))
+            for u in range(2):
+                acc = psum.tile([P, BANK], F32, name="acc%d%d%d" % (b, t, u), tag="bank%d" % (2 * t + u))
+                cols = slice(u * BANK, (u + 1) * BANK)
+                for i, (kind, a) in enumerate(order):
+                    if kind == "w4":
+                        c0 = ((b * 2 + a) * PACK + t) * P
+                        lhs = w4_w[:, 2 * c0 : 2 * (c0 + P)].bitcast(FP4X4)
+                        lhs_s = w4_s[:, c0 : c0 + P]
+                    else:
+                        c0 = (a * PACK + t) * P
+                        lhs = wd_w[b][:, c0 : c0 + P].bitcast(FP8X4)
+                        lhs_s = wd_s[b][:, c0 : c0 + P]
+                    nc.tensor.matmul_mx(
+                        out=acc[:], lhsT=lhs, lhsT_scale=lhs_s,
+                        rhs=v_w[a][:, cols].bitcast(FP8X4), rhs_scale=v_s[a][:, cols],
+                        start=(i == 0), stop=(i == len(order) - 1),
+                    )
+                nc.scalar.activation(out=act[b, t][:, cols], in_=acc[:], func=TANH, bias=per_row("bias", b, t))
+
+        def make_xa(b, t, picked, dst):
+            nc.vector.tensor_copy(picked, act[b, t][:].indirect(pos1_sb[:]))
+            nc.vector.tensor_scalar(dst, picked, per_row("gain", b, t), per_row("rest", b, t), ALU.mult, ALU.max)
+
+        def make_xb(b, t, picked, dst, lo, hi):
+            nc.vector.tensor_copy(picked, act[b, t][:].indirect(pos2_sb[:, lo // 16 : hi // 16]))
+            nc.vector.scalar_tensor_tensor(
+                dst, picked, per_row("gain", b, t), bed_sb[b][t][:, lo:hi], ALU.mult, ALU.add
+            )
+
+        def weave(copy, woven, rows):
+            copy(
+                out=woven.rearrange("p (c i t) -> p c t i", i=4, t=PACK),
+                in_=rows.rearrange("p t (c i) -> p c t i", i=4),
+            )
+
+        for t in range(PACK):
+            first_stage(0, t, (("wd", 0), ("w4", 0), ("w4", 1), ("wd", 1)))
+        prepare_wd(1, 0, "woven2")
+        prepare_wd(1, 1, "woven3")
+
+        wa_raw = [tile([P, PACK, N], F32, "wa_raw%d" % b, "raw%d" % b) for b in range(2)]
+        for b in range(2):
+            load_rows(wa_raw[b][:], wa, b, slice(0, N))
+        for t in range(PACK):
+            load_bed(1, t)
+        nc.sync.dma_start(
+            out=w8_w[:].rearrange("p (a c) -> p a c", a=2),
+            in_=w8_words.rearrange("a p c i -> p a (c i)").bitcast(I32),
+        )
+        load_scales(nc.sync, w8_s, w8_scales)
+        nc.sync.dma_start(out=base_sb[:], in_=base.rearrange("(n p) j -> p n j", p=P))
+
+        xa_rows = [tile([P, PACK, J], BF16, "xa_rows%d" % b) for b in range(2)]
+        xb_rows0 = tile([P, PACK, J], BF16, "xb_rows0")
+        for t in range(PACK):
+            if t == PACK - 1:
+                picked = tile([P, 2, J], F32, "picked_held", "woven3")
+            else:
+                picked = ring.tile([P, 2, J], F32, name="picked", tag="picked")
+            make_xa(0, t, picked[:, 0, :], xa_rows[0][:, t, :])
+            make_xb(0, t, picked[:, 1, :], xb_rows0[:, t, :], 0, J)
+
+        for t in range(PACK):
+            first_stage(1, t, (("w4", 0), ("w4", 1), ("wd", 0), ("wd", 1)))
+
+        for t in range(PACK):
+            picked = ring.tile([P, 2, J], F32, name="picked", tag="picked")
+            make_xa(1, t, picked[:, 0, :], xa_rows[1][:, t, :])
+        xb_rows1 = [tile([P, PACK, HALF], BF16, "xb_rows1%d" % u) for u in range(2)]
+        picked = tile([P, PACK, HALF], F32, "picked_first", "woven2")
+        for t in range(PACK):
+            make_xb(1, t, picked[:, t, :], xb_rows1[0][:, t, :], 0, HALF)
+
+        wa_w, wa_s = tile([P, 2 * N], U32, "wa_w"), tile([P, 2 * N], U8, "wa_s")
+        xa_w, xa_s = tile([P, 2 * J], U32, "xa_w"), tile([P, 2 * J], U8, "xa_s")
+        xb_w, xb_s = tile([P, 2 * J], U32, "xb_w"), tile([P, 2 * J], U8, "xb_s")
+
+        def prepare_wa(b, tag):
+            woven = tile([P, PACK * N], BF16, "wa_woven%d" % b, tag)
+            weave(nc.scalar.copy, woven[:], wa_raw[b][:])
+            quantise(wa_w[:, b * N : (b + 1) * N], wa_s[:, b * N : (b + 1) * N], woven[:])
+
+        def prepare_x(name, tag, copy, rows, words, scales, lo, width):
+            woven = tile([P, PACK * width], BF16, name, tag)
+            weave(copy, woven[:], rows[:])
+            quantise(words[:, lo : lo + width], scales[:, lo : lo + width], woven[:])
+
+        prepare_wa(0, "woven0")
+        prepare_x("xa_woven0", "held_a", nc.scalar.copy, xa_rows[0], xa_w, xa_s, 0, J)
+        prepare_wa(1, "woven1")
+        prepare_x("xa_woven1", "woven0", nc.scalar.copy, xa_rows[1], xa_w, xa_s, J, J)
+
+        picked = tile([P, PACK, HALF], F32, "picked_second", "woven0")
+        for t in range(PACK):
+            make_xb(1, t, picked[:, t, :], xb_rows1[1][:, t, :], HALF, J)
+
+        prepare_x("xb_woven0", "held_b", nc.scalar.copy, xb_rows0, xb_w, xb_s, 0, J)
+        prepare_x("xb_woven10", "woven1", nc.scalar.copy, xb_rows1[0], xb_w, xb_s, J, HALF)
+
+        ya = tile([P, 4, J], F32, "ya", "raw2")
+        for n in range(4):
+            acc = psum.tile([P, BANK], F32, name="ya_acc%d" % n, tag="bank%d" % n)
+            for b in range(2):
+                wcols = slice(b * N + n * P, b * N + (n + 1) * P)
+                xcols = slice(b * J, (b + 1) * J)
+                nc.tensor.matmul_mx(
+                    out=acc[:], lhsT=wa_w[:, wcols].bitcast(FP8X4), lhsT_scale=wa_s[:, wcols],
+                    rhs=xa_w[:, xcols].bitcast(FP8X4), rhs_scale=xa_s[:, xcols],
+                    start=(b == 0), stop=(b == 1),
+                )
+            nc.scalar.copy(out=ya[:, n, :], in_=acc[:])
+
+        prepare_x("xb_woven11", "woven2", nc.vector.tensor_copy, xb_rows1[1], xb_w, xb_s, J + HALF, HALF)
+
+        res = tile([P, 4, BANK], F32, "res", "raw3")
+        out_v = out.rearrange("(n p) j -> p n j", p=P)
+        for u in range(2):
+            jcols = slice(u * HALF, (u + 1) * HALF)
+            for g in range(2):
+                acc = psum.tile([P, BANK], F32, name="yb_acc%d%d" % (u, g), tag="bank%d" % (4 + 2 * u + g))
+                for b in range(2):
+                    for i in range(2):
+                        n = 2 * g + i
+                        wcols = slice(b * N + n * P, b * N + (n + 1) * P)
+                        xcols = slice(b * J + u * HALF, b * J + (u + 1) * HALF)
+                        nc.tensor.matmul_mx(
+                            out=acc[:, i * HALF : (i + 1) * HALF],
+                            lhsT=w8_w[:, wcols].bitcast(FP8X4), lhsT_scale=w8_s[:, wcols],
+                            rhs=xb_w[:, xcols].bitcast(FP8X4), rhs_scale=xb_s[:, xcols],
+                            start=(b == 0 and i == 0), stop=(b == 1 and i == 1),
+                        )
+                pair = slice(2 * g, 2 * g + 2)
+                part = res[:, 2 * u + g, :].rearrange("p (n j) -> p n j", n=2)
+                nc.vector.tensor_tensor(part, acc[:].rearrange("p (n j) -> p n j", n=2), ya[:, pair, jcols], ALU.mult)
+                nc.vector.tensor_tensor(part, part, base_sb[:, pair, jcols], ALU.max)
+                nc.sync.dma_start(out=out_v[:, pair, jcols], in_=part)

@@ -69,9 +69,8 @@ def tile_list_bed_window_scores_kernel(
         wd_last = tile([P, 2, PACK, KP // 2], F32, "wd_raw01", "raw1")
         wd_raw[1, 0] = tile([P, PACK, KP], F32, "wd_raw10", "raw2")
         wd_raw[1, 1] = tile([P, PACK, KP], F32, "wd_raw11", "raw3")
-        bed_sb = [[tile([P, J], F32, "bed%d%d" % (b, t)) for t in range(PACK)] for b in range(2)]
+        bed_sb = [[tile([P, J], F32, "bed0%d" % t)[:] for t in range(PACK)]]
         w8_w = tile([P, 2 * N], I32, "w8_w")
-        base_sb = tile([P, 4, J], F32, "base_sb")
 
         def load_tab(a):
             nc.sync.dma_start(out=tab_w[a][:], in_=tab_words[a].rearrange("p n i -> p (n i)").bitcast(I32))
@@ -84,7 +83,7 @@ def tile_list_bed_window_scores_kernel(
 
         def load_bed(b, t):
             rows = bed[b * KP : (b + 1) * KP, :].rearrange("(p t) j -> p t j", t=PACK)
-            nc.sync.dma_start(out=bed_sb[b][t][:], in_=rows[:, t, :])
+            nc.sync.dma_start(out=bed_sb[b][t], in_=rows[:, t, :])
 
         nc.sync.dma_start(offs_sb[:], offs)
         nc.sync.dma_start(out=tab_s[0:32, :].bitcast(I32), in_=tab_scales.rearrange("a q t -> (a q) t").bitcast(I32))
@@ -134,48 +133,48 @@ def tile_list_bed_window_scores_kernel(
                 )
         gather_words(0, 0, S)
 
-        w4_w = tile([P, 4 * KP * 2], U8, "w4_w", "held_b")
+        w4_w = {}
         w4_s = tile([P, 4 * KP], U8, "w4_s")
         nc.vector.tensor_copy(
             w4_s[:].rearrange("p (b a t m) -> p b a t m", b=2, a=2, t=PACK),
             w4s_raw[:].rearrange("p (a b m t) -> p b a t m", a=2, b=2, t=PACK),
         )
 
-        def deal_w4(b):
+        def deal_w4(b, tag):
+            w4_w[b] = tile([P, 2 * KP * 2], U8, "w4_w%d" % b, tag)
             nc.vector.tensor_copy(
-                w4_w[:, 2048 * b : 2048 * (b + 1)].bitcast(U16).rearrange("p (a t m) -> p a t m", a=2, t=PACK),
+                w4_w[b][:].bitcast(U16).rearrange("p (a t m) -> p a t m", a=2, t=PACK),
                 w4_raw[b][:].bitcast(U16).rearrange("p a (m t) -> p a t m", t=PACK),
             )
 
-        wd_w = [tile([P, 2 * KP], U32, "wd_w0"), tile([P, 2 * KP], U32, "wd_w1", "held_a")]
+        wd_w = [tile([P, 2 * KP], U32, "wd_w0", "late"), tile([P, 2 * KP], U32, "wd_w1", "held_a")]
         wd_s = [tile([P, 2 * KP], U8, "wd_s%d" % b) for b in range(2)]
 
         def quantise(words, scales, woven):
             nc.vector.quantize_mx(out=words.bitcast(FP8X4), scales=scales, in_=woven)
 
         def dealt_view(woven):
-            return woven[:].rearrange("p (t m j) -> p m j t", t=PACK, j=PACK)
+            return woven.rearrange("p (t m j) -> p m j t", t=PACK, j=PACK)
 
         def raw_view(raw):
             return raw.rearrange("p j (m t) -> p m j t", t=PACK)
 
-        def prepare_wd(b, a, tag):
-            woven = tile([P, PACK * KP], BF16, "wd_woven%d%d" % (b, a), tag)
+        def prepare_wd(b, a, woven):
             nc.scalar.copy(out=dealt_view(woven), in_=raw_view(wd_raw[b, a][:]))
             cols = slice(a * KP, (a + 1) * KP)
-            quantise(wd_w[b][:, cols], wd_s[b][:, cols], woven[:])
+            quantise(wd_w[b][:, cols], wd_s[b][:, cols], woven)
 
-        deal_w4(0)
-        prepare_wd(0, 0, "woven0")
+        deal_w4(0, "w4_w0")
+        prepare_wd(0, 0, tile([P, PACK * KP], BF16, "wd_woven00", "woven0")[:])
         gather_words(1, 0, S // 2)
         gather_words(1, S // 2, S)
         woven = tile([P, PACK * KP], BF16, "wd_woven01", "woven1")
-        nc.scalar.copy(out=dealt_view(woven)[:, 0:64], in_=raw_view(wd_last[:, 0]))
-        nc.vector.tensor_copy(out=dealt_view(woven)[:, 64:128], in_=raw_view(wd_last[:, 1]))
+        nc.scalar.copy(out=dealt_view(woven[:])[:, 0:64], in_=raw_view(wd_last[:, 0]))
+        nc.vector.tensor_copy(out=dealt_view(woven[:])[:, 64:128], in_=raw_view(wd_last[:, 1]))
         for t in range(PACK):
             cols = slice(KP + t * P, KP + (t + 1) * P)
             quantise(wd_w[0][:, cols], wd_s[0][:, cols], woven[:, t * KP : (t + 1) * KP])
-        deal_w4(1)
+        deal_w4(1, "woven1")
 
         act = {}
 
@@ -186,9 +185,9 @@ def tile_list_bed_window_scores_kernel(
                 cols = slice(u * BANK, (u + 1) * BANK)
                 for i, (kind, a) in enumerate(order):
                     if kind == "w4":
-                        c0 = ((b * 2 + a) * PACK + t) * P
-                        lhs = w4_w[:, 2 * c0 : 2 * (c0 + P)].bitcast(FP4X4)
-                        lhs_s = w4_s[:, c0 : c0 + P]
+                        c0 = (a * PACK + t) * P
+                        lhs = w4_w[b][:, 2 * c0 : 2 * (c0 + P)].bitcast(FP4X4)
+                        lhs_s = w4_s[:, 2 * KP * b + c0 : 2 * KP * b + c0 + P]
                     else:
                         c0 = (a * PACK + t) * P
                         lhs = wd_w[b][:, c0 : c0 + P].bitcast(FP8X4)
@@ -218,26 +217,29 @@ def tile_list_bed_window_scores_kernel(
 
         for t in range(PACK):
             first_stage(0, t, (("wd", 0), ("w4", 0), ("w4", 1), ("wd", 1)))
-        prepare_wd(1, 0, "woven2")
-        prepare_wd(1, 1, "woven3")
+        woven = tile([P, 2 * PACK * KP], BF16, "wd_woven1", "late")
+        for a in range(2):
+            prepare_wd(1, a, woven[:, a * PACK * KP : (a + 1) * PACK * KP])
 
-        wa_raw = [tile([P, PACK, N], F32, "wa_raw%d" % b, "raw%d" % b) for b in range(2)]
+        wa_raw = [tile([P, PACK, N], F32, "wa_raw%d" % b) for b in range(2)]
         for b in range(2):
             load_rows(wa_raw[b][:], wa, b, slice(0, N))
-        for t in range(PACK):
-            load_bed(1, t)
+        bed_late = tile([P, PACK, J], F32, "bed1", "raw1")
+        load_rows(bed_late[:], bed, 1, slice(0, J))
+        bed_sb.append([bed_late[:, t, :] for t in range(PACK)])
         nc.sync.dma_start(
             out=w8_w[:].rearrange("p (a c) -> p a c", a=2),
             in_=w8_words.rearrange("a p c i -> p a (c i)").bitcast(I32),
         )
         load_scales(nc.sync, w8_s, w8_scales)
+        base_sb = tile([P, 4, J], F32, "base_sb", "raw0")
         nc.sync.dma_start(out=base_sb[:], in_=base.rearrange("(n p) j -> p n j", p=P))
 
         xa_rows = [tile([P, PACK, J], BF16, "xa_rows%d" % b) for b in range(2)]
         xb_rows0 = tile([P, PACK, J], BF16, "xb_rows0")
         for t in range(PACK):
             if t == PACK - 1:
-                picked = tile([P, 2, J], F32, "picked_held", "woven3")
+                picked = tile([P, 2, J], F32, "picked_held", "late")
             else:
                 picked = ring.tile([P, 2, J], F32, name="picked", tag="picked")
             make_xa(0, t, picked[:, 0, :], xa_rows[0][:, t, :])
@@ -250,7 +252,7 @@ def tile_list_bed_window_scores_kernel(
             picked = ring.tile([P, 2, J], F32, name="picked", tag="picked")
             make_xa(1, t, picked[:, 0, :], xa_rows[1][:, t, :])
         xb_rows1 = [tile([P, PACK, HALF], BF16, "xb_rows1%d" % u) for u in range(2)]
-        picked = tile([P, PACK, HALF], F32, "picked_first", "woven2")
+        picked = tile([P, PACK, HALF], F32, "picked_first", "late")
         for t in range(PACK):
             make_xb(1, t, picked[:, t, :], xb_rows1[0][:, t, :], 0, HALF)
 
@@ -268,17 +270,17 @@ def tile_list_bed_window_scores_kernel(
             weave(copy, woven[:], rows[:])
             quantise(words[:, lo : lo + width], scales[:, lo : lo + width], woven[:])
 
-        prepare_wa(0, "woven0")
+        prepare_wa(0, "raw3")
         prepare_x("xa_woven0", "held_a", nc.scalar.copy, xa_rows[0], xa_w, xa_s, 0, J)
-        prepare_wa(1, "woven1")
+        prepare_wa(1, "raw2")
         prepare_x("xa_woven1", "woven0", nc.scalar.copy, xa_rows[1], xa_w, xa_s, J, J)
 
         picked = tile([P, PACK, HALF], F32, "picked_second", "woven0")
         for t in range(PACK):
             make_xb(1, t, picked[:, t, :], xb_rows1[1][:, t, :], HALF, J)
 
-        prepare_x("xb_woven0", "held_b", nc.scalar.copy, xb_rows0, xb_w, xb_s, 0, J)
-        prepare_x("xb_woven10", "woven1", nc.scalar.copy, xb_rows1[0], xb_w, xb_s, J, HALF)
+        prepare_x("xb_woven0", "woven1", nc.scalar.copy, xb_rows0, xb_w, xb_s, 0, J)
+        prepare_x("xb_woven10", "xb_woven10", nc.scalar.copy, xb_rows1[0], xb_w, xb_s, J, HALF)
 
         ya = tile([P, 4, J], F32, "ya", "raw2")
         for n in range(4):
@@ -293,7 +295,7 @@ def tile_list_bed_window_scores_kernel(
                 )
             nc.scalar.copy(out=ya[:, n, :], in_=acc[:])
 
-        prepare_x("xb_woven11", "woven2", nc.vector.tensor_copy, xb_rows1[1], xb_w, xb_s, J + HALF, HALF)
+        prepare_x("xb_woven11", "late", nc.vector.tensor_copy, xb_rows1[1], xb_w, xb_s, J + HALF, HALF)
 
         res = tile([P, 4, BANK], F32, "res", "raw3")
         out_v = out.rearrange("(n p) j -> p n j", p=P)

from contextlib import ExitStack

import concourse.mybir as mybir

K, H, N, T, S, J = 1024, 1024, 512, 4096, 1024, 512
FLOPS = 2 * (2 * K * H * S + 2 * H * N * J)

F32 = mybir.dt.float32
BF16 = mybir.dt.bfloat16
I32 = mybir.dt.int32
U32 = mybir.dt.uint32
U16 = mybir.dt.uint16
U8 = mybir.dt.uint8
FP8X4 = mybir.dt.float8_e4m3fn_x4
FP4X4 = mybir.dt.float4_e2m1fn_x4
ALU = mybir.AluOpType
TANH = mybir.ActivationFunctionType.Tanh

P = 128
PACK = 4
KP = P * PACK
BANK = 512
HALF = J // 2


def tile_list_bed_window_scores_kernel(
    tc, tab_words, tab_scales, offs, pos1, pos2, w4_words, w4_scales, wd, bias, gain, rest, bed, wa,
    w8_words, w8_scales, base, out,
):
    nc = tc.nc
    with ExitStack() as ctx:
        lists = ctx.enter_context(tc.tile_pool(name="lists", bufs=1))
        sb = ctx.enter_context(tc.tile_pool(name="sb", bufs=1))
        ring = ctx.enter_context(tc.tile_pool(name="ring", bufs=3))
        psum = ctx.enter_context(tc.psum_pool(name="psum", bufs=1))

        def tile(shape, dtype, name, tag=None):
            return sb.tile(shape, dtype, name=name, tag=tag or name, align_bytes=64)

        offs_sb = lists.tile([P, S // 16], U16, name="offs_sb")
        pos1_sb = lists.tile([P, J // 16], U16, name="pos1_sb")
        pos2_sb = lists.tile([P, J // 16], U16, name="pos2_sb")

        tab_s = tile([P, T], U8, "tab_s")
        v_s = [tile([P, S], U8, "v_s%d" % a) for a in range(2)]
        w4s_raw = tile([P, 2 * H], U8, "w4s_raw")
        w8_s = tile([P, 2 * N], U8, "w8_s")
        nc.vector.memset(w4s_raw[:].bitcast(I32), 0)
        nc.vector.memset(tab_s[64:128, :].bitcast(I32), 0)
        nc.gpsimd.memset(tab_s[32:64, :].bitcast(I32), 0)
        for a in range(2):
            nc.gpsimd.memset(v_s[a][:].bitcast(I32), 0)
        nc.gpsimd.memset(w8_s[:].bitcast(I32), 0)

        def load_scales(queue, plane, scales):
            for q in range(4):
                queue.dma_start(
                    out=plane[32 * q : 32 * q + 4, :].bitcast(I32).rearrange("r (a c) -> r a c", a=2),
                    in_=scales[:, 4 * q : 4 * q + 4, :].rearrange("a r c -> r a c").bitcast(I32),
                )

        def load_rows(dst, src, a, cols):
            nc.sync.dma_start(out=dst, in_=src[a * KP : (a + 1) * KP, cols].rearrange("(p j) c -> p j c", j=PACK))

        tab_w = [tile([P, T], I32, "tab_w%d" % a) for a in range(2)]
        w4_raw = [tile([P, 2, 256], I32, "w4_raw%d" % b) for b in range(2)]
        wd_raw = {}
        wd_raw[0, 0] = tile([P, PACK, KP], F32, "wd_raw00", "raw0")
        wd_last = tile([P, 2, PACK, KP // 2], F32, "wd_raw01", "raw1")
        wd_raw[1, 0] = tile([P, PACK, KP], F32, "wd_raw10", "raw2")
        wd_raw[1, 1] = tile([P, PACK, KP], F32, "wd_raw11", "raw3")
        bed_sb = [[tile([P, J], F32, "bed0%d" % t)[:] for t in range(PACK)]]
        w8_w = tile([P, 2 * N], I32, "w8_w")

        def load_tab(a):
            nc.sync.dma_start(out=tab_w[a][:], in_=tab_words[a].rearrange("p n i -> p (n i)").bitcast(I32))

        def load_w4(b):
            nc.sync.dma_start(
                out=w4_raw[b][:],
                in_=w4_words[:, :, 1024 * b : 1024 * (b + 1)].rearrange("a p c -> p a c").bitcast(I32),
            )

        def load_bed(b, t):
            rows = bed[b * KP : (b + 1) * KP, :].rearrange("(p t) j -> p t j", t=PACK)
            nc.sync.dma_start(out=bed_sb[b][t], in_=rows[:, t, :])

        nc.sync.dma_start(offs_sb[:], offs)
        nc.sync.dma_start(out=tab_s[0:32, :].bitcast(I32), in_=tab_scales.rearrange("a q t -> (a q) t").bitcast(I32))
        vec = {}

        def load_vec(name, src):
            vec[name] = tile([P, 2, PACK], F32, name + "_sb")
            nc.sync.dma_start(out=vec[name][:], in_=src.rearrange("(b p t) -> p b t", b=2, t=PACK))

        load_rows(wd_raw[0, 0][:], wd, 0, slice(0, KP))
        load_w4(0)
        load_vec("bias", bias)
        load_scales(nc.sync, w4s_raw, w4_scales)
        load_tab(0)
        load_tab(1)
        for u in range(2):
            load_rows(wd_last[:, u], wd, 1, slice(u * 256, (u + 1) * 256))
        nc.sync.dma_start(pos1_sb[:], pos1)
        nc.sync.dma_start(pos2_sb[:], pos2)
        load_vec("gain", gain)
        load_vec("rest", rest)
        load_w4(1)
        load_bed(0, 0)
        load_rows(wd_raw[1, 0][:], wd, 0, slice(KP, 2 * KP))
        load_bed(0, 1)
        load_rows(wd_raw[1, 1][:], wd, 1, slice(KP, 2 * KP))
        load_bed(0, 2)
        load_bed(0, 3)


        def per_row(name, b, t):
            return vec[name][:, b, t : t + 1]

        v_w = [tile([P, S], U32, "v_w%d" % a) for a in range(2)]

        def gather_words(a, lo, hi):
            window = tab_w[a][:].bitcast(U32)
            nc.vector.tensor_copy(v_w[a][:, lo:hi], window.indirect(offs_sb[:, lo // 16 : hi // 16]))

        picked_s = tile([P, S], U8, "picked_s")
        nc.vector.tensor_copy(picked_s[:], tab_s[:].indirect(offs_sb[:]))
        for a in range(2):
            for q in range(4):
                row = 16 * a + 4 * q
                nc.gpsimd.dma_start(
                    out=v_s[a][32 * q : 32 * q + 4, :].bitcast(I32), in_=picked_s[row : row + 4, :].bitcast(I32)
                )
        gather_words(0, 0, S)

        w4_w = {}
        w4_s = tile([P, 4 * KP], U8, "w4_s")
        nc.vector.tensor_copy(
            w4_s[:].rearrange("p (b a t m) -> p b a t m", b=2, a=2, t=PACK),
            w4s_raw[:].rearrange("p (a b m t) -> p b a t m", a=2, b=2, t=PACK),
        )

        def deal_w4(b, tag):
            w4_w[b] = tile([P, 2 * KP * 2], U8, "w4_w%d" % b, tag)
            nc.vector.tensor_copy(
                w4_w[b][:].bitcast(U16).rearrange("p (a t m) -> p a t m", a=2, t=PACK),
                w4_raw[b][:].bitcast(U16).rearrange("p a (m t) -> p a t m", t=PACK),
            )

        wd_w = [tile([P, 2 * KP], U32, "wd_w0", "late"), tile([P, 2 * KP], U32, "wd_w1", "held_a")]
        wd_s = [tile([P, 2 * KP], U8, "wd_s%d" % b) for b in range(2)]

        def quantise(words, scales, woven):
            nc.vector.quantize_mx(out=words.bitcast(FP8X4), scales=scales, in_=woven)

        def dealt_view(woven):
            return woven.rearrange("p (t m j) -> p m j t", t=PACK, j=PACK)

        def raw_view(raw):
            return raw.rearrange("p j (m t) -> p m j t", t=PACK)

        def prepare_wd(b, a, woven):
            nc.scalar.copy(out=dealt_view(woven), in_=raw_view(wd_raw[b, a][:]))
            cols = slice(a * KP, (a + 1) * KP)
            quantise(wd_w[b][:, cols], wd_s[b][:, cols], woven)

        deal_w4(0, "w4_w0")
        prepare_wd(0, 0, tile([P, PACK * KP], BF16, "wd_woven00", "woven0")[:])
        gather_words(1, 0, S // 2)
        gather_words(1, S // 2, S)
        woven = tile([P, PACK * KP], BF16, "wd_woven01", "woven1")
        nc.scalar.copy(out=dealt_view(woven[:])[:, 0:64], in_=raw_view(wd_last[:, 0]))
        nc.vector.tensor_copy(out=dealt_view(woven[:])[:, 64:128], in_=raw_view(wd_last[:, 1]))
        for t in range(PACK):
            cols = slice(KP + t * P, KP + (t + 1) * P)
            quantise(wd_w[0][:, cols], wd_s[0][:, cols], woven[:, t * KP : (t + 1) * KP])
        deal_w4(1, "woven1")

        act = {}

        def first_stage(b, t, order):
            act[b, t] = tile([P, S], F32, "act%d%d" % (b, t))
            for u in range(2):
                acc = psum.tile([P, BANK], F32, name="acc%d%d%d" % (b, t, u), tag="bank%d" % (2 * t + u))
                cols = slice(u * BANK, (u + 1) * BANK)
                for i, (kind, a) in enumerate(order):
                    if kind == "w4":
                        c0 = (a * PACK + t) * P
                        lhs = w4_w[b][:, 2 * c0 : 2 * (c0 + P)].bitcast(FP4X4)
                        lhs_s = w4_s[:, 2 * KP * b + c0 : 2 * KP * b + c0 + P]
                    else:
                        c0 = (a * PACK + t) * P
                        lhs = wd_w[b][:, c0 : c0 + P].bitcast(FP8X4)
                        lhs_s = wd_s[b][:, c0 : c0 + P]
                    nc.tensor.matmul_mx(
                        out=acc[:], lhsT=lhs, lhsT_scale=lhs_s,
                        rhs=v_w[a][:, cols].bitcast(FP8X4), rhs_scale=v_s[a][:, cols],
                        start=(i == 0), stop=(i == len(order) - 1),
                    )
                nc.scalar.activation(out=act[b, t][:, cols], in_=acc[:], func=TANH, bias=per_row("bias", b, t))

        def make_xa(b, t, picked, dst):
            nc.vector.tensor_copy(picked, act[b, t][:].indirect(pos1_sb[:]))
            nc.vector.tensor_scalar(dst, picked, per_row("gain", b, t), per_row("rest", b, t), ALU.mult, ALU.max)

        def make_xb(b, t, picked, dst, lo, hi):
            nc.vector.tensor_copy(picked, act[b, t][:].indirect(pos2_sb[:, lo // 16 : hi // 16]))
            nc.vector.scalar_tensor_tensor(
                dst, picked, per_row("gain", b, t), bed_sb[b][t][:, lo:hi], ALU.mult, ALU.add
            )

        def weave(copy, woven, rows):
            copy(
                out=woven.rearrange("p (c i t) -> p c t i", i=4, t=PACK),
                in_=rows.rearrange("p t (c i) -> p c t i", i=4),
            )

        for t in range(PACK):
            first_stage(0, t, (("wd", 0), ("w4", 0), ("w4", 1), ("wd", 1)))
        woven = tile([P, 2 * PACK * KP], BF16, "wd_woven1", "late")
        for a in range(2):
            prepare_wd(1, a, woven[:, a * PACK * KP : (a + 1) * PACK * KP])

        wa_raw = [tile([P, PACK, N], F32, "wa_raw%d" % b) for b in range(2)]
        for b in range(2):
            load_rows(wa_raw[b][:], wa, b, slice(0, N))
        bed_late = tile([P, PACK, J], F32, "bed1", "raw1")
        load_rows(bed_late[:], bed, 1, slice(0, J))
        bed_sb.append([bed_late[:, t, :] for t in range(PACK)])
        nc.sync.dma_start(
            out=w8_w[:].rearrange("p (a c) -> p a c", a=2),
            in_=w8_words.rearrange("a p c i -> p a (c i)").bitcast(I32),
        )
        load_scales(nc.sync, w8_s, w8_scales)
        base_sb = tile([P, 4, J], F32, "base_sb", "raw0")
        nc.sync.dma_start(out=base_sb[:], in_=base.rearrange("(n p) j -> p n j", p=P))

        xa_rows = [tile([P, PACK, J], BF16, "xa_rows%d" % b) for b in range(2)]
        xb_rows0 = tile([P, PACK, J], BF16, "xb_rows0")
        for t in range(PACK):
            if t == PACK - 1:
                picked = tile([P, 2, J], F32, "picked_held", "late")
            else:
                picked = ring.tile([P, 2, J], F32, name="picked", tag="picked")
            make_xa(0, t, picked[:, 0, :], xa_rows[0][:, t, :])
            make_xb(0, t, picked[:, 1, :], xb_rows0[:, t, :], 0, J)

        for t in range(PACK):
            first_stage(1, t, (("w4", 0), ("w4", 1), ("wd", 0), ("wd", 1)))

        for t in range(PACK):
            picked = ring.tile([P, 2, J], F32, name="picked", tag="picked")
            make_xa(1, t, picked[:, 0, :], xa_rows[1][:, t, :])
        xb_rows1 = [tile([P, PACK, HALF], BF16, "xb_rows1%d" % u) for u in range(2)]
        picked = tile([P, PACK, HALF], F32, "picked_first", "late")
        for t in range(PACK):
            make_xb(1, t, picked[:, t, :], xb_rows1[0][:, t, :], 0, HALF)

        wa_w, wa_s = tile([P, 2 * N], U32, "wa_w"), tile([P, 2 * N], U8, "wa_s")
        xa_w, xa_s = tile([P, 2 * J], U32, "xa_w"), tile([P, 2 * J], U8, "xa_s")
        xb_w, xb_s = tile([P, 2 * J], U32, "xb_w"), tile([P, 2 * J], U8, "xb_s")

        def prepare_wa(b, tag):
            woven = tile([P, PACK * N], BF16, "wa_woven%d" % b, tag)
            weave(nc.scalar.copy, woven[:], wa_raw[b][:])
            quantise(wa_w[:, b * N : (b + 1) * N], wa_s[:, b * N : (b + 1) * N], woven[:])

        def prepare_x(name, tag, copy, rows, words, scales, lo, width):
            woven = tile([P, PACK * width], BF16, name, tag)
            weave(copy, woven[:], rows[:])
            quantise(words[:, lo : lo + width], scales[:, lo : lo + width], woven[:])

        prepare_wa(0, "raw3")
        prepare_x("xa_woven0", "held_a", nc.scalar.copy, xa_rows[0], xa_w, xa_s, 0, J)
        prepare_wa(1, "raw2")
        prepare_x("xa_woven1", "woven0", nc.scalar.copy, xa_rows[1], xa_w, xa_s, J, J)

        picked = tile([P, PACK, HALF], F32, "picked_second", "woven0")
        for t in range(PACK):
            make_xb(1, t, picked[:, t, :], xb_rows1[1][:, t, :], HALF, J)

        prepare_x("xb_woven0", "woven1", nc.scalar.copy, xb_rows0, xb_w, xb_s, 0, J)
        prepare_x("xb_woven10", "xb_woven10", nc.scalar.copy, xb_rows1[0], xb_w, xb_s, J, HALF)

        ya = tile([P, 4, J], F32, "ya", "raw2")
        for n in range(4):
            acc = psum.tile([P, BANK], F32, name="ya_acc%d" % n, tag="bank%d" % n)
            for b in range(2):
                wcols = slice(b * N + n * P, b * N + (n + 1) * P)
                xcols = slice(b * J, (b + 1) * J)
                nc.tensor.matmul_mx(
                    out=acc[:], lhsT=wa_w[:, wcols].bitcast(FP8X4), lhsT_scale=wa_s[:, wcols],
                    rhs=xa_w[:, xcols].bitcast(FP8X4), rhs_scale=xa_s[:, xcols],
                    start=(b == 0), stop=(b == 1),
                )
            nc.scalar.copy(out=ya[:, n, :], in_=acc[:])

        prepare_x("xb_woven11", "late", nc.vector.tensor_copy, xb_rows1[1], xb_w, xb_s, J + HALF, HALF)

        res = tile([P, 4, BANK], F32, "res", "raw3")
        out_v = out.rearrange("(n p) j -> p n j", p=P)
        for u in range(2):
            jcols = slice(u * HALF, (u + 1) * HALF)
            for g in range(2):
                acc = psum.tile([P, BANK], F32, name="yb_acc%d%d" % (u, g), tag="bank%d" % (4 + 2 * u + g))
                for b in range(2):
                    for i in range(2):
                        n = 2 * g + i
                        wcols = slice(b * N + n * P, b * N + (n + 1) * P)
                        xcols = slice(b * J + u * HALF, b * J + (u + 1) * HALF)
                        nc.tensor.matmul_mx(
                            out=acc[:, i * HALF : (i + 1) * HALF],
                            lhsT=w8_w[:, wcols].bitcast(FP8X4), lhsT_scale=w8_s[:, wcols],
                            rhs=xb_w[:, xcols].bitcast(FP8X4), rhs_scale=xb_s[:, xcols],
                            start=(b == 0 and i == 0), stop=(b == 1 and i == 1),
                        )
                pair = slice(2 * g, 2 * g + 2)
                part = res[:, 2 * u + g, :].rearrange("p (n j) -> p n j", n=2)
                nc.vector.tensor_tensor(part, acc[:].rearrange("p (n j) -> p n j", n=2), ya[:, pair, jcols], ALU.mult)
                nc.vector.tensor_tensor(part, part, base_sb[:, pair, jcols], ALU.max)
                nc.sync.dma_start(out=out_v[:, pair, jcols], in_=part)
